import numpy as np, ml_dtypes
CORES = [25,29,65,69,153,157,193,197]
N = 8
T, EL, CAP, CAPP = 4096, 2, 1920, 512
E = N * EL
def entries(a): return a.T.reshape(-1)
def pack(v, P): return np.ascontiguousarray(np.asarray(v, np.int32).reshape(-1, P).T)
def lists(rng, how):
    if how == "uniform": return {"ex": np.stack([pack(rng.permutation(np.repeat(np.arange(E), CAPP))[:T], 16) for r in range(N)])}
    R = np.arange(N)[:, None]; c = rng.permutation(E); C = np.zeros((N, E), np.int64)
    if how == "bands":
        a = c % N; C = CAPP * ((R >= a) & (R <= a + CAP // CAPP)); C[a, np.arange(E)] = np.where(c < N, CAPP, rng.integers(1, CAPP + 1, E))
    if how == "full":
        g = T // CAPP; C[:, c[:g]] = CAPP; C[:, c[:g // 2]] = rng.integers(CAPP // 2, CAPP + 1, (N, g // 2))
    if how in ("skew", "sorted"):
        V = np.full((N, 3), CAP // N); V[:, 0] = rng.integers(2, CAP // N + 1, N); h = rng.integers(1, N - 2); V[h, 0] = 0; V[h + 1, 0] = 1; V[rng.integers(N), 1:] += CAP % N; V[rng.integers(N), 2] += 1
        W = rng.random((N, E)) ** 4 + 1e-9; W[:, c[:3]] = 0
        C = np.minimum(((T - T // 8 - V.sum(axis=1, keepdims=True)) * W / W.sum(axis=1, keepdims=True)).astype(np.int64), CAPP); C[:, c[:3]] = V
    if how == "thin":
        C = rng.integers(0, CAP // N + 1, (N, E)); C[1] = 1; C[[0, N // 2, N - 1]] = 0
    X = np.stack([rng.permutation(np.concatenate([np.repeat(np.arange(E), C[r]), np.full(T - C[r].sum(), -1)])) for r in range(N)])
    if how == "sorted": X = np.sort(X, axis=1); X[1::2] = X[1::2, ::-1].copy()
    return {"ex": np.stack([pack(v, 16) for v in X])}
def blank(d):
    for r in range(0, N, 2):
        u, i = np.unique(entries(d["ex"][r])[::-1], return_index=True); d["x"][r][:, T - 1 - i[u >= 0]] = 0
def setup_inputs(rng):
    return dict({"x": rng.standard_normal((N, 128, T), dtype=np.float32).astype(ml_dtypes.bfloat16)}, **lists(rng, "uniform"))
def setup_inputs_bands(rng):
    d = setup_inputs(rng); d.update(lists(rng, "bands"))
    for k in ("x",): d[k] = (d[k].astype(np.float32) * 1048576.0).astype(d[k].dtype)
    blank(d)
    return d
def setup_inputs_full(rng):
    d = setup_inputs(rng); d.update(lists(rng, "full"))
    for k in ("x",): d[k] = (d[k].astype(np.float32) * (1 / 1024.0)).astype(d[k].dtype)
    blank(d)
    return d
def setup_inputs_skew(rng):
    d = setup_inputs(rng); d.update(lists(rng, "skew"))
    blank(d)
    return d
def setup_inputs_sorted(rng):
    d = setup_inputs(rng); d.update(lists(rng, "sorted"))
    blank(d)
    return d
def setup_inputs_thin(rng):
    d = setup_inputs(rng); d.update(lists(rng, "thin"))
    blank(d)
    return d
def check_inputs(x):
    bad = []
    if x["ex"].min() < -1 or x["ex"].max() >= E: bad.append("ex out of range")
    if max(int(np.bincount(entries(a)[entries(a) >= 0], minlength=E).max()) for a in x["ex"]) > CAPP: bad.append("more than CAPP tokens of one rank choose one expert")
    return bad
def reference(x, ex):
    X = np.concatenate(list(x), axis=1); e = np.concatenate([entries(a) for a in ex])
    k = np.nonzero(e >= 0)[0]; o = k[np.argsort(e[k], kind="stable")]; s = e[o]
    p = np.arange(len(o)) - np.searchsorted(s, s)
    Y = np.zeros((128, E * CAP), x.dtype); m = p < CAP; Y[:, CAP * s[m] + p[m]] = X[:, o[m]]
    return {"y": np.stack([Y[:, EL * CAP * r:EL * CAP * (r + 1)] for r in range(N)])}

@@ -1,0 +1,354 @@
+from concourse.bass import DstId, RemoteDMATransfer
+from concourse.mybir import AluOpType, ActivationFunctionType, AxisListType
+
+WORLD, N, COLS, EL, CAP, CAPP = 256, 8, 4096, 2, 1920, 512
+LANDW = N * CAPP + CAP
+HALF = COLS // 2
+NC = CAP // 16
+
+
+def sb(n, dtype="float32"):
+    return ("sbuf", [128, n], dtype)
+
+
+PS = ("psum", [128, 512], "float32")
+SCRATCH = {
+    "ext": sb(256, "int32"),
+    "xs": sb(COLS, "bfloat16"),
+    "PI": sb(4, "int32"), "PF": sb(4),
+    "EB": sb(2), "W": sb(8),
+    "i240": sb(240), "mk": sb(128), "mI": sb(128), "JC": sb(256), "A": sb(256, "bfloat16"), "kk": sb(16),
+    "mask16": sb(16, "bfloat16"), "Z2": sb(240, "float16"), "Z3": sb(240, "bfloat16"), "Zq": sb(144, "bfloat16"),
+    "ones": sb(128, "bfloat16"), "B": sb(128, "bfloat16"), "GT": sb(128, "bfloat16"), "L": sb(128, "bfloat16"),
+    "I16": sb(128, "float16"), "Jneg": sb(256, "float16"), "JT": sb(32, "float16"),
+    "O": sb(256, "bfloat16"), "S": sb(264, "bfloat16"), "V": sb(256, "float16"),
+    "Cn": sb(16, "bfloat16"), "CS": sb(16),
+    "dat": sb(512, "bfloat16"), "win": sb(512 + 8 * CAPP, "bfloat16"),
+    "soff": sb(32, "uint16"), "goff": sb(256, "uint16"),
+    "sb": sb(6 * CAPP, "bfloat16"),
+    "CT": sb(4 * N),
+    "land0": sb(LANDW, "bfloat16"), "land1": sb(LANDW, "bfloat16"),
+    "P0": sb(NC), "P1": sb(NC), "P0h": sb(NC, "float16"), "mq": sb(128), "Zr": sb(128, "float16"),
+    "M1": sb(8), "M2": sb(8), "TT": sb(32), "SD": sb(8),
+    "R": sb(2 * NC, "float16"), "ytab": sb(2 * NC, "uint16"), "ys": sb(EL * CAP, "bfloat16"),
+    "pos": PS, "tgt": PS, "cntp": PS, "lstA": PS, "lstB": PS, "tabp": PS,
+}
+SEMAPHORES = ["sv", "ss", "sp", "sg", "lex", "lx0", "lx1", "rex", "rx", "cnt", "arr0", "arr1", "sent", "stored"]
+CACHE = {}
+
+
+def roles(T, topo):
+    cores = T.cores
+
+    def place(c):
+        return (topo.host(c), topo.chip(c))
+    chips = {}
+    for r, c in enumerate(cores):
+        chips.setdefault(place(c), []).append(r)
+    out, helpers = {}, {}
+    for r, c in enumerate(cores):
+        plane = own = None
+        for pl, grp in chips.items():
+            d = cores[grp[0]]
+            if pl == place(c):
+                own = grp
+            elif topo.same_plane(c, d):
+                plane = grp
+            else:
+                for h in range(WORLD):
+                    if h in cores or h in out or topo.die(h) != topo.die(c) or not topo.may_write(h, d):
+                        continue
+                    if topo.host(c) == topo.host(d):
+                        fits = topo.mates(h, d) and topo.same_plane(c, h)
+                    else:
+                        fits = place(h) == place(c)
+                    if fits:
+                        out[h] = (r, grp, None)
+                        helpers.setdefault(r, []).append(h)
+                        break
+        out[c] = (r, plane, own)
+    return out, helpers
+
+
+def bits(m):
+    return [1 << i for i in range(16) if m >> i & 1]
+
+
+def rank_program(g, core, T, topo):
+    if "roles" not in CACHE:
+        CACHE["roles"] = roles(T, topo)
+    table, helpers = CACHE["roles"]
+    if core not in table:
+        return
+    r, far, own = table[core]
+    cores = T.cores
+    is_rank = own is not None
+    A, X, F = AluOpType, AxisListType.X, ActivationFunctionType
+    q = {"v": g.vector, "s": g.scalar, "p": g.tensor, "g": g, "y": g.sync}
+    n, seen = {}, {}
+
+    def did(name, ins, k=1):
+        ins.then_inc(T.sem[name], k)
+        n[name] = n.get(name, 0) + k
+        return (name, n[name])
+
+    def need(k, *marks):
+        for name, val in marks:
+            if seen.get((k, name), 0) < val:
+                q[k].wait_ge(T.sem[name], val)
+                seen[(k, name)] = val
+
+    def v(ins):
+        return did("sv", ins)
+
+    def s(ins):
+        return did("ss", ins)
+
+    def pe(ins):
+        return did("sp", ins)
+
+    def gp(ins):
+        return did("sg", ins)
+
+    def send(parts):
+        ts = []
+        for d, a, b, sem, eng in parts:
+            rid, pnc = topo.addr(d, core)
+            n["sent"] = n.get("sent", 0) + len(eng)
+            ts.append(RemoteDMATransfer(dst_ids=[DstId(rid=rid, pnc=pnc)], dma_engine_mask=sum(eng), remote_sem=sem, src=a, dst=b))
+        g.remote_dma_fused(ts, local_sem=T.sem.sent)
+
+    vec, sca, ten = g.vector, g.scalar, g.tensor
+    mm = ten.matmul
+    off = bits(topo.mask(core, cores[far[0]]))
+    hlf = len(off) // 2
+    if is_rank:
+        mate = [d for d in own if d != r][0]
+        on = [b for b in bits(topo.mask(core, cores[mate])) if b not in off]
+        hs = helpers[r]
+        h_near = [h for h in hs if topo.host(h) == topo.host(core) and topo.chip(h) == topo.chip(core)][0]
+        h_far = [h for h in hs if h != h_near][0]
+
+    if is_rank:
+        for k in range(8):
+            eng = g.sync if k % 2 == 0 else g.scalar
+            EXL = did("lex", eng.dma_start(T.ext[16 * k:16 * k + 16, :], T.ex[:, :]), 16)
+        XL = []
+        for h in range(2):
+            for j, eng in enumerate((g.sync, g.scalar)):
+                a = HALF * h + HALF // 2 * j
+                m = did("lx%d" % h, eng.dma_start(T.xs[:, a:a + HALF // 2], T.x[:, a:a + HALF // 2]), 16)
+            XL.append(m)
+    else:
+        n["rex"] = len(off)
+        n["rx"] = 2 * len(off)
+        EXL, XL = ("rex", n["rex"]), [("rx", n["rx"])]
+
+    ok = {"allow_small_or_imprecise_dtypes": True}
+    g_pi = gp(g.iota(T.PI[:, 0:1], [[1, 1]], 0, 1))
+    g_mk = gp(g.iota(T.mk[:, :], [[1, 8], [0, 16]], 0, 0, **ok))
+    g_mI = gp(g.iota(T.mI[:, :], [[1, 128]], 0, 0, **ok))
+    g_JC = gp(g.iota(T.JC[:, :], [[0, 8], [-16, 32]], 0, 0, **ok))
+    g_240 = gp(g.iota(T.i240[:, :], [[1, 240]], -112, 0, **ok))
+    if is_rank:
+        need("g", EXL)
+        send([(h_far, T.ext[:, :], T.ext[:, :], T.sem.rex, off), (h_near, T.ext[:, :], T.ext[:, :], T.sem.rex, on)])
+    g_A = gp(g.iota(T.A[:, :], [[1, 256]], 0, 0, **ok))
+    g_kk = gp(g.iota(T.kk[:, :], [[2, 4], [1, 4]], 0, 0, **ok))
+    if is_rank:
+        for h in range(2):
+            need("g", XL[h])
+            w = T.xs[:, HALF * h:HALF * (h + 1)]
+            send([(h_far, w, w, T.sem.rx, off), (h_near, w, w, T.sem.rx, on)])
+        gp(g.iota(T.P0[:, :], [[16, NC]], 0, 0, **ok))
+        g_mq = gp(g.iota(T.mq[:, :], [[0, 8], [1, 16]], 0, 0, **ok))
+
+    NK = 8 if is_rank else 4
+    v_win = v(vec.memset(T.win[:, 512:512 + 4 * CAPP], 0.0))
+    if is_rank:
+        need("s", v_win)
+        s_win = s(sca.activation(T.win[:, 512 + 4 * CAPP:512 + 8 * CAPP], T.win[:, 512:512 + 4 * CAPP], F.Copy))
+    v(vec.memset(T.EB[0:64, 0:1], float(EL * far[0])))
+    v(vec.memset(T.EB[64:128, 0:1], float(EL * own[0] - 4) if is_rank else -100.0))
+    v(vec.memset(T.ones[:, :], 1.0))
+    v(vec.memset(T.Zq[:, :], 0.0))
+    v(vec.memset(T.S[:, 0:1], 0.0))
+    need("v", g_pi)
+    v(vec.tensor_scalar(T.PI[:, 1:2], T.PI[:, 0:1], 4, None, A.arith_shift_right))
+    m = v(vec.tensor_scalar(T.PI[:, 2:3], T.PI[:, 0:1], 15, None, A.bitwise_and))
+    need("v", m)
+    m = v(vec.tensor_copy(T.PF[:, 0:3], T.PI[:, 0:3]))
+    need("v", m)
+    pf, pk, pq, kw = T.PF[:, 0:1], T.PF[:, 1:2], T.PF[:, 2:3], T.PF[:, 3:4]
+    v(vec.tensor_scalar(kw, pk, float(CAPP), float(CAPP), A.mult, A.add))
+    v_e = v(vec.tensor_tensor(T.EB[:, 1:2], T.EB[:, 0:1], pk, A.add))
+    w0, w1, w2, w12, wt, wu, wg = [T.W[:, j:j + 1] for j in range(7)]
+    v(vec.tensor_scalar(w0, pq, 0.0, None, A.is_equal))
+    v(vec.tensor_scalar(w1, pq, 1.0, None, A.is_equal))
+    m = v(vec.tensor_scalar(w2, pq, 2.0, None, A.is_equal))
+    need("v", g_mI)
+    v(vec.tensor_scalar(T.B[:, :], T.mk[:, :], pk, None, A.is_equal))
+    m2 = v(vec.tensor_scalar(T.GT[:, :], T.mI[:, :], pf, None, A.is_gt))
+    v(vec.tensor_scalar(T.I16[:, :], T.mI[:, :], pf, None, A.is_equal))
+    need("v", m)
+    v(vec.tensor_tensor(w12, w1, w2, A.add))
+    v(vec.tensor_scalar(wt, pk, 512.0, w2, A.mult, A.mult))
+    m = v(vec.tensor_scalar(wu, w1, 256.0, w0, A.mult, A.add))
+    need("v", m2)
+    v(vec.tensor_tensor(T.L[:, :], T.GT[:, :], T.B[:, :], A.mult))
+    need("v", g_JC)
+    v(vec.tensor_scalar(T.Jneg[:, :], T.JC[:, :], pq, None, A.subtract))
+    v_JT = v(vec.tensor_scalar(T.JT[:, :], T.JC[:, 0:32], -1.0, pq, A.mult, A.add))
+    need("v", m)
+    m = v(vec.tensor_tensor(wg, wt, wu, A.add))
+    need("v", g_240)
+    v(vec.tensor_scalar(T.Z2[:, :], T.i240[:, :], pq, None, A.is_equal))
+    v(vec.tensor_scalar(T.Z3[:, :], T.i240[:, :], pq, kw, A.is_equal, A.mult))
+    need("v", m)
+    v(vec.tensor_scalar(T.Zq[:, 15::16], T.ones[:, 0:9], wg, None, A.mult))
+    need("v", g_kk)
+    v(vec.tensor_scalar(T.dat[:, 0:256], T.A[:, :], w0, w2, A.mult, A.add))
+    v(vec.tensor_scalar(T.dat[:, 256:512], T.A[:, :], w0, w12, A.mult, A.add))
+    v(vec.tensor_scalar(T.mask16[:, :], T.kk[:, :], pk, None, A.is_equal))
+
+    need("v", EXL, v_e)
+    v_O = v(vec.tensor_scalar(T.O[:, :], T.ext[:, :], T.EB[:, 1:2], None, A.is_equal))
+    need("v", v_O)
+    v_S = v(vec.tensor_tensor_scan(T.S[:, 1:257], T.O[:, :], T.O[:, :], 0.0, A.add, A.max))
+    need("v", v_S)
+    v(vec.tensor_scalar(T.Cn[:, :], T.mask16[:, :], T.S[:, 256:257], None, A.mult))
+
+    need("p", v_JT)
+    mm(T.tgt[:, 0:32], T.I16[:, :], T.JT[:, :], True, False)
+    mm(T.pos[:, 0:256], T.I16[:, :], T.Jneg[:, :], True, False)
+    need("p", v_O)
+    mm(T.pos[:, 0:256], T.L[:, :], T.O[:, :], False, False)
+    need("p", v_S)
+    p_pos = pe(mm(T.pos[:, 0:256], T.B[:, :], T.S[:, 0:256], False, True))
+    for k in range(8):
+        mm(T.tgt[:, 0:32], T.Z3[:, 112 - 16 * k:240 - 16 * k], T.O[:, 32 * k:32 * k + 32], False, False)
+    need("v", p_pos)
+    v_V = v(vec.tensor_tensor(T.V[:, :], T.O[:, :], T.pos[:, 0:256], A.mult))
+    need("p", v_V)
+    for k in range(8):
+        ins = mm(T.tgt[:, 0:32], T.Z2[:, 112 - 16 * k:240 - 16 * k], T.V[:, 32 * k:32 * k + 32], False, k == 7)
+    p_tgt = pe(ins)
+    p_cnt = pe(mm(T.cntp[:, 0:16], T.ones[:, :], T.Cn[:, :], True, True))
+    need("v", p_tgt)
+    v_so = v(vec.tensor_copy(T.soff[:, :], T.tgt[:, 0:32]))
+    need("v", v_so)
+    if is_rank:
+        need("v", s_win)
+    v_sc = v(vec.tensor_copy(T.win[:, 0:512 + NK * CAPP].indirect(T.soff[:, 0:32]), T.dat[:, :]))
+
+    need("s", p_cnt)
+    s_CS = s(sca.activation(T.CS[:, :], T.cntp[:, 0:16], F.Copy))
+    if is_rank:
+        i = 2 + own.index(r)
+        s_own = s(sca.activation(T.CT[:, 4 * r:4 * r + 4], T.cntp[:, 4 * i:4 * i + 4], F.Copy))
+    need("g", s_CS)
+    slot = T.CT[:, 4 * r:4 * r + 4]
+    parts = [(cores[far[i]], T.CS[:, 4 * i:4 * i + 4], slot, T.sem.cnt, off[hlf * i:hlf * (i + 1)]) for i in range(2)]
+    if is_rank:
+        i = 2 + own.index(mate)
+        parts.append((cores[mate], T.CS[:, 4 * i:4 * i + 4], slot, T.sem.cnt, on))
+    send(parts)
+
+    need("p", v_sc)
+    for bank in (T.lstA, T.lstB)[:NK // 4]:
+        a = 512 if bank is T.lstA else 512 + 4 * CAPP
+        for j in range(16):
+            ins = mm(bank[:, 0:128], T.Zq[:, 15 - j:143 - j], T.win[:, a + j:a + 4 * CAPP:16], j == 0, j == 15)
+        m = pe(ins)
+        if a == 512:
+            p_A = m
+        else:
+            p_B = m
+
+    def gather_v(out, w, o):
+        return v(vec.tensor_copy(out, w.indirect(o)))
+
+    def gather_s(out, w, o):
+        return s(sca.activation(out, w.indirect(o), F.Identity, bias=-0.0, scale=1.0))
+
+    xs = T.xs[:, :]
+    need("v", p_A)
+    v_go = v(vec.tensor_copy(T.goff[:, 0:128], T.lstA[:, 0:128]))
+    need("v", v_go, *XL)
+    need("s", v_go, *XL)
+    pair = []
+    for e in range(2):
+        a = gather_v(T.sb[:, CAPP * e:CAPP * (e + 1)], xs, T.goff[:, 32 * e:32 * e + 32])
+        b = gather_s(T.sb[:, CAPP * (2 + e):CAPP * (3 + e)], xs, T.goff[:, 64 + 32 * e:96 + 32 * e])
+        pair.append((a, b))
+    land, arr = [T.land0, T.land1], [T.sem.arr0, T.sem.arr1]
+    for e in range(2):
+        need("g", *pair[e])
+        send([(cores[far[i]], T.sb[:, CAPP * (2 * i + e):CAPP * (2 * i + e + 1)], land[e][:, CAPP * r:CAPP * (r + 1)],
+               arr[e], off[hlf * i:hlf * (i + 1)]) for i in range(2)])
+    if is_rank:
+        need("v", p_B)
+        v_gb = v(vec.tensor_copy(T.goff[:, 128:256], T.lstB[:, 0:128]))
+        need("v", v_gb)
+        need("s", v_gb)
+        im, io = 128 + 64 * own.index(mate), 128 + 64 * own.index(r)
+        a = gather_v(T.sb[:, 4 * CAPP:5 * CAPP], xs, T.goff[:, im:im + 32])
+        b = gather_s(T.sb[:, 5 * CAPP:6 * CAPP], xs, T.goff[:, im + 32:im + 64])
+        for e, mark in enumerate((a, b)):
+            need("g", mark)
+            send([(cores[mate], T.sb[:, CAPP * (4 + e):CAPP * (5 + e)], land[e][:, CAPP * r:CAPP * (r + 1)], arr[e], on)])
+        own_mark = [gather_v(T.land0[:, CAPP * r:CAPP * (r + 1)], xs, T.goff[:, io:io + 32]),
+                    gather_s(T.land1[:, CAPP * r:CAPP * (r + 1)], xs, T.goff[:, io + 32:io + 64])]
+
+        for e in range(2):
+            v(vec.memset(land[e][:, N * CAPP:LANDW], 0.0))
+        need("v", g_mq)
+        i8 = T.i240[:, 112:120]
+        v(vec.tensor_scalar(T.M1[:, :], i8, pk, None, A.is_le))
+        v(vec.tensor_scalar(T.M2[:, :], i8, pk, -1.0, A.is_equal, A.mult))
+        v(vec.tensor_scalar(T.Zr[:, :], T.mq[:, :], pq, None, A.is_equal))
+        v(vec.tensor_scalar(T.P0h[:, :], T.P0[:, :], pq, None, A.add))
+        m = v(vec.tensor_scalar(T.P1[:, :], T.P0[:, :], pq, None, A.add))
+        n_src = 2 * 3 * hlf + len(on)
+        n["cnt"] = n["arr0"] = n["arr1"] = n_src
+        need("v", m, s_own, ("cnt", n_src))
+        for e in range(2):
+            v(vec.tensor_tensor(T.TT[:, 16 * e:16 * e + 8], T.CT[:, e::4], T.M1[:, :], A.mult))
+            m = v(vec.tensor_tensor(T.TT[:, 16 * e + 8:16 * e + 16], T.CT[:, e::4], T.M2[:, :], A.mult))
+        need("v", m)
+        for e in range(2):
+            v(vec.tensor_reduce(T.SD[:, 2 * e + 4:2 * e + 5], T.TT[:, 16 * e + 8:16 * e + 16], X, A.add))
+            m = v(vec.tensor_reduce(T.SD[:, 2 * e:2 * e + 1], T.TT[:, 16 * e:16 * e + 8], X, A.add))
+        need("v", m)
+        for e in range(2):
+            m = v(vec.tensor_scalar(T.SD[:, 2 * e + 1:2 * e + 2], T.SD[:, 2 * e + 4:2 * e + 5], float(CAPP), None, A.add))
+        need("v", m)
+        for e in range(2):
+            m = v(vec.tensor_scalar(T.R[:, NC * e:NC * (e + 1)], T.P1[:, :], T.SD[:, 2 * e:2 * e + 1],
+                                    T.SD[:, 2 * e + 1:2 * e + 2], A.is_ge, A.mult))
+        need("p", m)
+        for e in range(2):
+            mm(T.tabp[:, NC * e:NC * (e + 1)], T.I16[:, :], T.P0h[:, :], True, False)
+            ins = mm(T.tabp[:, NC * e:NC * (e + 1)], T.Zr[:, :], T.R[:, NC * e:NC * (e + 1)], False, True)
+        p_t = pe(ins)
+        need("v", p_t)
+        v_yt = v(vec.tensor_copy(T.ytab[:, :], T.tabp[:, 0:2 * NC]))
+        need("v", v_yt)
+        need("s", v_yt)
+
+        for e in range(2):
+            need("v", own_mark[e], ("arr%d" % e, n_src))
+            need("s", own_mark[e], ("arr%d" % e, n_src))
+            a = 0
+            for w in ([CAP // 2], [CAP // 4, CAP // 4])[e]:
+                for k, gather in enumerate((gather_v, gather_s)):
+                    c0 = CAP // 2 * k + a
+                    lo, hi = CAP * e + c0, CAP * e + c0 + w
+                    m = gather(T.ys[:, lo:hi], land[e][:, :], T.ytab[:, lo // 16:hi // 16])
+                    need("y", m)
+                    did("stored", g.sync.dma_start(T.y[:, lo:hi], T.ys[:, lo:hi]), 16)
+                a += w
+
+    for name in SEMAPHORES:
+        if n.get(name, 0):
+            need("g", (name, n[name]))

@@ -2,8 +2,9 @@ from concourse.bass import DstId, RemoteDMATransfer
 from concourse.mybir import AluOpType, ActivationFunctionType, AxisListType
 
 WORLD, N, COLS, EL, CAP, CAPP = 256, 8, 4096, 2, 1920, 512
-LANDW = N * CAPP + CAP
-HALF = COLS // 2
+LANDW = N * CAPP + 16
+PIECES = (0, 1536, 2816, 4096)
+NP = len(PIECES) - 1
 NC = CAP // 16
 
 
@@ -13,27 +14,27 @@ def sb(n, dtype="float32"):
 
 PS = ("psum", [128, 512], "float32")
 SCRATCH = {
-    "ext": sb(256, "int32"),
+    "ext": sb(256, "int32"), "exs": sb(128, "bfloat16"),
     "xs": sb(COLS, "bfloat16"),
-    "PI": sb(4, "int32"), "PF": sb(4),
-    "EB": sb(2), "W": sb(8),
-    "i240": sb(240), "mk": sb(128), "mI": sb(128), "JC": sb(256), "A": sb(256, "bfloat16"), "kk": sb(16),
-    "mask16": sb(16, "bfloat16"), "Z2": sb(240, "float16"), "Z3": sb(240, "bfloat16"), "Zq": sb(144, "bfloat16"),
+    "PI": sb(8, "int32"), "PF": sb(8), "W": sb(16),
+    "i176": sb(176), "mk": sb(128), "JC": sb(128), "A": sb(128, "bfloat16"), "kk": sb(8),
+    "mask8": sb(8, "bfloat16"), "Z2": sb(176, "float16"), "Z3": sb(176, "bfloat16"), "Zq": sb(144, "bfloat16"),
     "ones": sb(128, "bfloat16"), "B": sb(128, "bfloat16"), "GT": sb(128, "bfloat16"), "L": sb(128, "bfloat16"),
-    "I16": sb(128, "float16"), "Jneg": sb(256, "float16"), "JT": sb(32, "float16"),
-    "O": sb(256, "bfloat16"), "S": sb(264, "bfloat16"), "V": sb(256, "float16"),
-    "Cn": sb(16, "bfloat16"), "CS": sb(16),
-    "dat": sb(512, "bfloat16"), "win": sb(512 + 8 * CAPP, "bfloat16"),
-    "soff": sb(32, "uint16"), "goff": sb(256, "uint16"),
+    "I16": sb(128, "float16"), "Jneg": sb(128, "float16"), "JT": sb(32, "float16"),
+    "O": sb(128, "bfloat16"), "S": sb(136, "bfloat16"), "V": sb(128, "float16"),
+    "Cn": sb(8, "bfloat16"), "CS": sb(8),
+    "dat": sb(512, "bfloat16"), "win": sb(5 * CAPP, "bfloat16"),
+    "soff": sb(32, "uint16"), "goff": sb(128, "uint16"), "gpl": sb(128, "uint16"),
     "sb": sb(6 * CAPP, "bfloat16"),
     "CT": sb(4 * N),
     "land0": sb(LANDW, "bfloat16"), "land1": sb(LANDW, "bfloat16"),
-    "P0": sb(NC), "P1": sb(NC), "P0h": sb(NC, "float16"), "mq": sb(128), "Zr": sb(128, "float16"),
-    "M1": sb(8), "M2": sb(8), "TT": sb(32), "SD": sb(8),
+    "P0": sb(2 * NC), "P1": sb(NC), "P0h": sb(2 * NC, "float16"), "mq": sb(128), "r32": sb(4 * N), "Zr": sb(128, "float16"),
+    "M1": sb(4 * N), "M2": sb(4 * N), "TT": sb(8 * N), "SD": sb(8),
     "R": sb(2 * NC, "float16"), "ytab": sb(2 * NC, "uint16"), "ys": sb(EL * CAP, "bfloat16"),
     "pos": PS, "tgt": PS, "cntp": PS, "lstA": PS, "lstB": PS, "tabp": PS,
 }
-SEMAPHORES = ["sv", "ss", "sp", "sg", "lex", "lx0", "lx1", "rex", "rx", "cnt", "arr0", "arr1", "sent", "stored"]
+SEMAPHORES = (["sv", "ss", "sp", "sg", "lex", "rex", "cnt", "arr0", "arr1", "lst0", "lst1", "sent", "stored"]
+              + ["lx%d" % h for h in range(NP)] + ["rx%d" % h for h in range(NP)])
 CACHE = {}
 
 
@@ -45,29 +46,29 @@ def roles(T, topo):
     chips = {}
     for r, c in enumerate(cores):
         chips.setdefault(place(c), []).append(r)
-    out, helpers = {}, {}
+    out, who = {}, {}
+
+    def take(part, r, grp, fits):
+        c = cores[r]
+        for h in range(WORLD):
+            if h not in cores and h not in out and topo.die(h) == topo.die(c) and topo.may_write(h, cores[grp[0]]) and fits(h):
+                out[h], who[part, r] = (part, r, grp), h
+                return
+    plane = {}
     for r, c in enumerate(cores):
-        plane = own = None
         for pl, grp in chips.items():
             d = cores[grp[0]]
             if pl == place(c):
-                own = grp
+                out[c] = ("rank", r, grp)
             elif topo.same_plane(c, d):
-                plane = grp
+                plane[r] = grp
+            elif topo.host(c) == topo.host(d):
+                take("far", r, grp, lambda h: topo.mates(h, d) and topo.same_plane(c, h))
             else:
-                for h in range(WORLD):
-                    if h in cores or h in out or topo.die(h) != topo.die(c) or not topo.may_write(h, d):
-                        continue
-                    if topo.host(c) == topo.host(d):
-                        fits = topo.mates(h, d) and topo.same_plane(c, h)
-                    else:
-                        fits = place(h) == place(c)
-                    if fits:
-                        out[h] = (r, grp, None)
-                        helpers.setdefault(r, []).append(h)
-                        break
-        out[c] = (r, plane, own)
-    return out, helpers
+                take("near", r, grp, lambda h: place(h) == place(c))
+    for r, c in enumerate(cores):
+        take("list", r, plane[r], lambda h: place(h) == place(c))
+    return out, who
 
 
 def bits(m):
@@ -77,12 +78,12 @@ def bits(m):
 def rank_program(g, core, T, topo):
     if "roles" not in CACHE:
         CACHE["roles"] = roles(T, topo)
-    table, helpers = CACHE["roles"]
+    table, who = CACHE["roles"]
     if core not in table:
         return
-    r, far, own = table[core]
+    part, r, grp = table[core]
     cores = T.cores
-    is_rank = own is not None
+    is_rank, is_list = part == "rank", part == "list"
     A, X, F = AluOpType, AxisListType.X, ActivationFunctionType
     q = {"v": g.vector, "s": g.scalar, "p": g.tensor, "g": g, "y": g.sync}
     n, seen = {}, {}
@@ -120,150 +121,178 @@ def rank_program(g, core, T, topo):
 
     vec, sca, ten = g.vector, g.scalar, g.tensor
     mm = ten.matmul
-    off = bits(topo.mask(core, cores[far[0]]))
+    far, near, lister = who["far", r], who["near", r], who["list", r]
+    c_r = cores[r]
+    off_r = bits(topo.mask(c_r, far))
+    on_r = [b for b in bits(topo.mask(c_r, near)) if b not in off_r]
+    half = len(on_r) // 2
+    off = off_r if is_rank else bits(topo.mask(core, cores[grp[0]]))
     hlf = len(off) // 2
-    if is_rank:
-        mate = [d for d in own if d != r][0]
-        on = [b for b in bits(topo.mask(core, cores[mate])) if b not in off]
-        hs = helpers[r]
-        h_near = [h for h in hs if topo.host(h) == topo.host(core) and topo.chip(h) == topo.chip(core)][0]
-        h_far = [h for h in hs if h != h_near][0]
+    mate = [d for d in table[c_r][2] if d != r][0]
 
+    XP = [T.xs[:, PIECES[h]:PIECES[h + 1]] for h in range(NP)]
+    XL = []
     if is_rank:
         for k in range(8):
             eng = g.sync if k % 2 == 0 else g.scalar
             EXL = did("lex", eng.dma_start(T.ext[16 * k:16 * k + 16, :], T.ex[:, :]), 16)
-        XL = []
-        for h in range(2):
-            for j, eng in enumerate((g.sync, g.scalar)):
-                a = HALF * h + HALF // 2 * j
-                m = did("lx%d" % h, eng.dma_start(T.xs[:, a:a + HALF // 2], T.x[:, a:a + HALF // 2]), 16)
-            XL.append(m)
+        for h in range(NP):
+            eng = g.sync if h % 2 == 0 else g.scalar
+            XL.append(did("lx%d" % h, eng.dma_start(XP[h], T.x[:, PIECES[h]:PIECES[h + 1]]), 16))
     else:
-        n["rex"] = len(off)
-        n["rx"] = 2 * len(off)
-        EXL, XL = ("rex", n["rex"]), [("rx", n["rx"])]
+        n["rex"] = len(off_r) if part == "far" else half
+        for h in range(0 if is_list else NP):
+            n["rx%d" % h] = len(off_r) if part == "far" else len(on_r) if h else len(off_r + on_r)
+            XL.append(("rx%d" % h, n["rx%d" % h]))
+
+    v(vec.memset(T.win[:, CAPP:5 * CAPP], 0.0))
+    if is_rank:
+        need("v", EXL)
+        v(vec.tensor_copy(T.exs[0:64, :], T.ext[0:64, 0::2]))
+        EXS = v(vec.tensor_copy(T.exs[64:128, :], T.ext[64:128, 1::2]))
+    else:
+        EXS = ("rex", n["rex"])
 
     ok = {"allow_small_or_imprecise_dtypes": True}
-    g_pi = gp(g.iota(T.PI[:, 0:1], [[1, 1]], 0, 1))
-    g_mk = gp(g.iota(T.mk[:, :], [[1, 8], [0, 16]], 0, 0, **ok))
-    g_mI = gp(g.iota(T.mI[:, :], [[1, 128]], 0, 0, **ok))
-    g_JC = gp(g.iota(T.JC[:, :], [[0, 8], [-16, 32]], 0, 0, **ok))
-    g_240 = gp(g.iota(T.i240[:, :], [[1, 240]], -112, 0, **ok))
-    if is_rank:
-        need("g", EXL)
-        send([(h_far, T.ext[:, :], T.ext[:, :], T.sem.rex, off), (h_near, T.ext[:, :], T.ext[:, :], T.sem.rex, on)])
-    g_A = gp(g.iota(T.A[:, :], [[1, 256]], 0, 0, **ok))
-    g_kk = gp(g.iota(T.kk[:, :], [[2, 4], [1, 4]], 0, 0, **ok))
-    if is_rank:
-        for h in range(2):
+
+    def x_on(h):
+        w, sem = XP[h], T.sem["rx%d" % h]
+        if is_rank:
             need("g", XL[h])
-            w = T.xs[:, HALF * h:HALF * (h + 1)]
-            send([(h_far, w, w, T.sem.rx, off), (h_near, w, w, T.sem.rx, on)])
-        gp(g.iota(T.P0[:, :], [[16, NC]], 0, 0, **ok))
+            if h == 0:
+                send([(near, w, w, sem, off_r + on_r)])
+            else:
+                send([(far, w, w, sem, off_r), (near, w, w, sem, on_r)])
+        elif part == "near" and h == 0:
+            need("g", XL[h])
+            send([(far, w, w, sem, off_r)])
+
+    g_pi = gp(g.iota(T.PI[:, 0:1], [[1, 1]], 0, 1))
+    gp(g.iota(T.i176[:, :], [[1, 176]], -48, 0, **ok))
+    g_mk = gp(g.iota(T.mk[:, :], [[0, 2], [1, 4], [0, 16]], 0, 0, **ok))
+    if is_rank:
+        need("g", EXS)
+        ex = T.exs[:, :]
+        send([(far, ex, ex, T.sem.rex, off_r), (near, ex, ex, T.sem.rex, on_r[:half]), (lister, ex, ex, T.sem.rex, on_r[half:])])
+        x_on(0)
+        x_on(1)
+    g_JC = gp(g.iota(T.JC[:, :], [[0, 4], [-16, 32]], 0, 0, **ok))
+    g_A = gp(g.iota(T.A[:, :], [[32, 8], [1, 16]], 0, 0, **ok))
+    g_kk = gp(g.iota(T.kk[:, :], [[1, 2], [2, 4]], 0, 0, **ok))
+    for h in range(2 if is_rank else 0, NP):
+        x_on(h)
+    if is_rank:
+        gp(g.iota(T.P0[:, :], [[0, 2], [16, NC]], 0, 0, **ok))
+        gp(g.iota(T.r32[:, :], [[1, N], [0, 4]], 0, 0, **ok))
         g_mq = gp(g.iota(T.mq[:, :], [[0, 8], [1, 16]], 0, 0, **ok))
 
-    NK = 8 if is_rank else 4
-    v_win = v(vec.memset(T.win[:, 512:512 + 4 * CAPP], 0.0))
-    if is_rank:
-        need("s", v_win)
-        s_win = s(sca.activation(T.win[:, 512 + 4 * CAPP:512 + 8 * CAPP], T.win[:, 512:512 + 4 * CAPP], F.Copy))
-    v(vec.memset(T.EB[0:64, 0:1], float(EL * far[0])))
-    v(vec.memset(T.EB[64:128, 0:1], float(EL * own[0] - 4) if is_rank else -100.0))
     v(vec.memset(T.ones[:, :], 1.0))
     v(vec.memset(T.Zq[:, :], 0.0))
     v(vec.memset(T.S[:, 0:1], 0.0))
     need("v", g_pi)
-    v(vec.tensor_scalar(T.PI[:, 1:2], T.PI[:, 0:1], 4, None, A.arith_shift_right))
-    m = v(vec.tensor_scalar(T.PI[:, 2:3], T.PI[:, 0:1], 15, None, A.bitwise_and))
+    pi = T.PI[:, 0:1]
+    v(vec.tensor_scalar(T.PI[:, 1:2], pi, 4, None, A.arith_shift_right))
+    v(vec.tensor_scalar(T.PI[:, 2:3], pi, 15, None, A.bitwise_and))
+    v(vec.tensor_scalar(T.PI[:, 3:4], pi, 79, None, A.bitwise_and))
+    v(vec.tensor_scalar(T.PI[:, 4:5], pi, 4, 3, A.arith_shift_right, A.bitwise_and))
+    v(vec.tensor_scalar(T.PI[:, 5:6], pi, 4, 1, A.arith_shift_right, A.bitwise_and))
+    v(vec.tensor_scalar(T.PI[:, 6:7], pi, 5, 1, A.arith_shift_right, A.bitwise_and))
+    m = v(vec.tensor_scalar(T.PI[:, 7:8], pi, 6, None, A.arith_shift_right))
     need("v", m)
-    m = v(vec.tensor_copy(T.PF[:, 0:3], T.PI[:, 0:3]))
+    m = v(vec.tensor_copy(T.PF[:, :], T.PI[:, :]))
     need("v", m)
-    pf, pk, pq, kw = T.PF[:, 0:1], T.PF[:, 1:2], T.PF[:, 2:3], T.PF[:, 3:4]
-    v(vec.tensor_scalar(kw, pk, float(CAPP), float(CAPP), A.mult, A.add))
-    v_e = v(vec.tensor_tensor(T.EB[:, 1:2], T.EB[:, 0:1], pk, A.add))
-    w0, w1, w2, w12, wt, wu, wg = [T.W[:, j:j + 1] for j in range(7)]
+    pf, pr, pq, ph, pk, p_i, p_e, p_h = [T.PF[:, j:j + 1] for j in range(8)]
+    w0, w1, w2, kw, eb, ta, tb, wu, wg, d1, d2, d3 = [T.W[:, j:j + 1] for j in range(12)]
     v(vec.tensor_scalar(w0, pq, 0.0, None, A.is_equal))
     v(vec.tensor_scalar(w1, pq, 1.0, None, A.is_equal))
-    m = v(vec.tensor_scalar(w2, pq, 2.0, None, A.is_equal))
-    need("v", g_mI)
+    v(vec.tensor_scalar(w2, pq, 2.0, None, A.is_equal))
+    v(vec.tensor_scalar(kw, pk, float(CAPP), float(CAPP), A.mult, A.add))
+    v(vec.tensor_scalar(eb, p_i, 2.0, p_e, A.mult, A.add))
+    m = v(vec.tensor_scalar(ta, pk, 1024.0, None, A.mult))
+    need("v", g_mk)
+    mI = T.i176[:, 48:176]
     v(vec.tensor_scalar(T.B[:, :], T.mk[:, :], pk, None, A.is_equal))
-    m2 = v(vec.tensor_scalar(T.GT[:, :], T.mI[:, :], pf, None, A.is_gt))
-    v(vec.tensor_scalar(T.I16[:, :], T.mI[:, :], pf, None, A.is_equal))
+    v(vec.tensor_scalar(T.GT[:, :], mI, pf, None, A.is_gt))
+    v(vec.tensor_scalar(T.I16[:, :], mI, pf, None, A.is_equal))
+    v(vec.tensor_scalar(T.Z2[:, :], T.i176[:, :], ph, None, A.is_equal))
     need("v", m)
-    v(vec.tensor_tensor(w12, w1, w2, A.add))
-    v(vec.tensor_scalar(wt, pk, 512.0, w2, A.mult, A.mult))
-    m = v(vec.tensor_scalar(wu, w1, 256.0, w0, A.mult, A.add))
-    need("v", m2)
+    v(vec.tensor_scalar(T.Z3[:, :], T.i176[:, :], ph, kw, A.is_equal, A.mult))
+    v(vec.tensor_scalar(tb, p_h, 16.0, ta, A.mult, A.add))
+    v(vec.tensor_scalar(wu, w1, 256.0, w0, A.mult, A.add))
+    v(vec.tensor_scalar(d1, w1, 1.0, w2, A.mult, A.add))
+    v(vec.tensor_scalar(d2, w1, 2.0, w2, A.mult, A.add))
+    m = v_d = v(vec.tensor_scalar(d3, w1, 3.0, w2, A.mult, A.add))
+    need("v", m)
     v(vec.tensor_tensor(T.L[:, :], T.GT[:, :], T.B[:, :], A.mult))
+    m = v(vec.tensor_scalar(wg, tb, w2, wu, A.mult, A.add))
     need("v", g_JC)
     v(vec.tensor_scalar(T.Jneg[:, :], T.JC[:, :], pq, None, A.subtract))
     v_JT = v(vec.tensor_scalar(T.JT[:, :], T.JC[:, 0:32], -1.0, pq, A.mult, A.add))
     need("v", m)
-    m = v(vec.tensor_tensor(wg, wt, wu, A.add))
-    need("v", g_240)
-    v(vec.tensor_scalar(T.Z2[:, :], T.i240[:, :], pq, None, A.is_equal))
-    v(vec.tensor_scalar(T.Z3[:, :], T.i240[:, :], pq, kw, A.is_equal, A.mult))
-    need("v", m)
     v(vec.tensor_scalar(T.Zq[:, 15::16], T.ones[:, 0:9], wg, None, A.mult))
     need("v", g_kk)
-    v(vec.tensor_scalar(T.dat[:, 0:256], T.A[:, :], w0, w2, A.mult, A.add))
-    v(vec.tensor_scalar(T.dat[:, 256:512], T.A[:, :], w0, w12, A.mult, A.add))
-    v(vec.tensor_scalar(T.mask16[:, :], T.kk[:, :], pk, None, A.is_equal))
+    v_c = v(vec.tensor_scalar(T.mask8[:, :], T.kk[:, :], pk, None, A.is_equal))
+    need("s", g_A, v_d)
+    for d, bias in enumerate((w2, d1, d2, d3)):
+        s_dat = s(sca.activation(T.dat[:, 128 * d:128 * d + 128], T.A[:, :], F.Identity, bias=bias, scale=w0))
 
-    need("v", EXL, v_e)
-    v_O = v(vec.tensor_scalar(T.O[:, :], T.ext[:, :], T.EB[:, 1:2], None, A.is_equal))
+    need("v", EXS, v_c)
+    v_O = v(vec.tensor_scalar(T.O[:, :], T.exs[:, :], float(EL * grp[0]), eb, A.subtract, A.is_equal))
     need("v", v_O)
-    v_S = v(vec.tensor_tensor_scan(T.S[:, 1:257], T.O[:, :], T.O[:, :], 0.0, A.add, A.max))
+    v_S = v(vec.tensor_tensor_scan(T.S[:, 1:129], T.O[:, :], T.O[:, :], 0.0, A.add, A.max))
     need("v", v_S)
-    v(vec.tensor_scalar(T.Cn[:, :], T.mask16[:, :], T.S[:, 256:257], None, A.mult))
+    v(vec.tensor_scalar(T.Cn[:, :], T.mask8[:, :], T.S[:, 128:129], None, A.mult))
 
     need("p", v_JT)
     mm(T.tgt[:, 0:32], T.I16[:, :], T.JT[:, :], True, False)
-    mm(T.pos[:, 0:256], T.I16[:, :], T.Jneg[:, :], True, False)
+    mm(T.pos[:, 0:128], T.I16[:, :], T.Jneg[:, :], True, False)
     need("p", v_O)
-    mm(T.pos[:, 0:256], T.L[:, :], T.O[:, :], False, False)
+    mm(T.pos[:, 0:128], T.L[:, :], T.O[:, :], False, False)
     need("p", v_S)
-    p_pos = pe(mm(T.pos[:, 0:256], T.B[:, :], T.S[:, 0:256], False, True))
-    for k in range(8):
-        mm(T.tgt[:, 0:32], T.Z3[:, 112 - 16 * k:240 - 16 * k], T.O[:, 32 * k:32 * k + 32], False, False)
+    p_pos = pe(mm(T.pos[:, 0:128], T.B[:, :], T.S[:, 0:128], False, True))
+    for b in range(4):
+        mm(T.tgt[:, 0:32], T.Z3[:, 48 - 16 * b:176 - 16 * b], T.O[:, 32 * b:32 * b + 32], False, False)
     need("v", p_pos)
-    v_V = v(vec.tensor_tensor(T.V[:, :], T.O[:, :], T.pos[:, 0:256], A.mult))
+    v_V = v(vec.tensor_tensor(T.V[:, :], T.O[:, :], T.pos[:, 0:128], A.mult))
     need("p", v_V)
-    for k in range(8):
-        ins = mm(T.tgt[:, 0:32], T.Z2[:, 112 - 16 * k:240 - 16 * k], T.V[:, 32 * k:32 * k + 32], False, k == 7)
+    for b in range(4):
+        ins = mm(T.tgt[:, 0:32], T.Z2[:, 48 - 16 * b:176 - 16 * b], T.V[:, 32 * b:32 * b + 32], False, b == 3)
     p_tgt = pe(ins)
-    p_cnt = pe(mm(T.cntp[:, 0:16], T.ones[:, :], T.Cn[:, :], True, True))
+    p_cnt = pe(mm(T.cntp[:, 0:8], T.ones[:, :], T.Cn[:, :], True, True))
     need("v", p_tgt)
     v_so = v(vec.tensor_copy(T.soff[:, :], T.tgt[:, 0:32]))
-    need("v", v_so)
-    if is_rank:
-        need("v", s_win)
-    v_sc = v(vec.tensor_copy(T.win[:, 0:512 + NK * CAPP].indirect(T.soff[:, 0:32]), T.dat[:, :]))
+    need("v", v_so, s_dat)
+    v_sc = v(vec.tensor_copy(T.win[:, :].indirect(T.soff[:, 0:32]), T.dat[:, :]))
 
     need("s", p_cnt)
-    s_CS = s(sca.activation(T.CS[:, :], T.cntp[:, 0:16], F.Copy))
-    if is_rank:
-        i = 2 + own.index(r)
-        s_own = s(sca.activation(T.CT[:, 4 * r:4 * r + 4], T.cntp[:, 4 * i:4 * i + 4], F.Copy))
-    need("g", s_CS)
+    s_CS = s(sca.activation(T.CS[:, :], T.cntp[:, 0:8], F.Copy))
     slot = T.CT[:, 4 * r:4 * r + 4]
-    parts = [(cores[far[i]], T.CS[:, 4 * i:4 * i + 4], slot, T.sem.cnt, off[hlf * i:hlf * (i + 1)]) for i in range(2)]
     if is_rank:
-        i = 2 + own.index(mate)
-        parts.append((cores[mate], T.CS[:, 4 * i:4 * i + 4], slot, T.sem.cnt, on))
-    send(parts)
+        io, im = grp.index(r), grp.index(mate)
+        s_own = s(sca.activation(slot, T.cntp[:, 4 * io:4 * io + 4], F.Copy))
+    need("g", s_CS)
+    if is_rank:
+        send([(cores[mate], T.CS[:, 4 * im:4 * im + 4], slot, T.sem.cnt, on_r)])
+    else:
+        send([(cores[grp[i]], T.CS[:, 4 * i:4 * i + 4], slot, T.sem.cnt, off[hlf * i:hlf * (i + 1)]) for i in range(2)])
 
     need("p", v_sc)
-    for bank in (T.lstA, T.lstB)[:NK // 4]:
-        a = 512 if bank is T.lstA else 512 + 4 * CAPP
+    p_l = []
+    for e, bank in enumerate((T.lstA, T.lstB)):
+        a = CAPP + 2 * CAPP * e
         for j in range(16):
-            ins = mm(bank[:, 0:128], T.Zq[:, 15 - j:143 - j], T.win[:, a + j:a + 4 * CAPP:16], j == 0, j == 15)
-        m = pe(ins)
-        if a == 512:
-            p_A = m
-        else:
-            p_B = m
+            ins = mm(bank[:, 0:64], T.Zq[:, 15 - j:143 - j], T.win[:, a + j:a + 2 * CAPP:16], j == 0, j == 15)
+        p_l.append(pe(ins))
+
+    if is_rank:
+        v(vec.memset(T.land0[:, N * CAPP:LANDW], 0.0))
+        v(vec.memset(T.land1[:, N * CAPP:LANDW], 0.0))
+        need("v", g_mq)
+        v(vec.tensor_scalar(T.M1[:, :], T.r32[:, :], pr, None, A.is_le))
+        v(vec.tensor_scalar(T.M2[:, :], T.r32[:, :], pr, -1.0, A.is_equal, A.mult))
+        v(vec.tensor_scalar(T.Zr[:, :], T.mq[:, :], pq, None, A.is_equal))
+        v(vec.tensor_scalar(T.P1[:, :], T.P0[:, 0:NC], pq, None, A.add))
+        v_rc = v(vec.tensor_scalar(T.P0h[:, :], T.P0[:, :], pq, None, A.add))
 
     def gather_v(out, w, o):
         return v(vec.tensor_copy(out, w.indirect(o)))
@@ -272,67 +301,77 @@ def rank_program(g, core, T, topo):
         return s(sca.activation(out, w.indirect(o), F.Identity, bias=-0.0, scale=1.0))
 
     xs = T.xs[:, :]
-    need("v", p_A)
-    v_go = v(vec.tensor_copy(T.goff[:, 0:128], T.lstA[:, 0:128]))
-    need("v", v_go, *XL)
-    need("s", v_go, *XL)
-    pair = []
-    for e in range(2):
-        a = gather_v(T.sb[:, CAPP * e:CAPP * (e + 1)], xs, T.goff[:, 32 * e:32 * e + 32])
-        b = gather_s(T.sb[:, CAPP * (2 + e):CAPP * (3 + e)], xs, T.goff[:, 64 + 32 * e:96 + 32 * e])
-        pair.append((a, b))
     land, arr = [T.land0, T.land1], [T.sem.arr0, T.sem.arr1]
-    for e in range(2):
-        need("g", *pair[e])
-        send([(cores[far[i]], T.sb[:, CAPP * (2 * i + e):CAPP * (2 * i + e + 1)], land[e][:, CAPP * r:CAPP * (r + 1)],
-               arr[e], off[hlf * i:hlf * (i + 1)]) for i in range(2)])
-    if is_rank:
-        need("v", p_B)
-        v_gb = v(vec.tensor_copy(T.goff[:, 128:256], T.lstB[:, 0:128]))
-        need("v", v_gb)
-        need("s", v_gb)
-        im, io = 128 + 64 * own.index(mate), 128 + 64 * own.index(r)
-        a = gather_v(T.sb[:, 4 * CAPP:5 * CAPP], xs, T.goff[:, im:im + 32])
-        b = gather_s(T.sb[:, 5 * CAPP:6 * CAPP], xs, T.goff[:, im + 32:im + 64])
-        for e, mark in enumerate((a, b)):
-            need("g", mark)
-            send([(cores[mate], T.sb[:, CAPP * (4 + e):CAPP * (5 + e)], land[e][:, CAPP * r:CAPP * (r + 1)], arr[e], on)])
-        own_mark = [gather_v(T.land0[:, CAPP * r:CAPP * (r + 1)], xs, T.goff[:, io:io + 32]),
-                    gather_s(T.land1[:, CAPP * r:CAPP * (r + 1)], xs, T.goff[:, io + 32:io + 64])]
+    own_mark = []
 
+    def lists(e):
+        need("v", p_l[e])
+        return v(vec.tensor_copy(T.goff[:, 64 * e:64 * e + 64], (T.lstA, T.lstB)[e][:, 0:64]))
+
+    def list_of(buf, e, i):
+        return buf[:, 64 * e + 32 * i:64 * e + 32 * i + 32]
+
+    def sb_at(j):
+        return T.sb[:, CAPP * j:CAPP * (j + 1)]
+
+    def slot_at(e):
+        return land[e][:, CAPP * r:CAPP * (r + 1)]
+
+    def pair(e, buf, mark, dests):
+        need("v", mark, *XL)
+        need("s", mark, *XL)
+        a = gather_v(sb_at(2 * e), xs, list_of(buf, e, 0))
+        b = gather_s(sb_at(2 * e + 1), xs, list_of(buf, e, 1))
+        need("g", a, b)
+        send([(cores[dests[i]], sb_at(2 * e + i), slot_at(e), arr[e], off[hlf * i:hlf * (i + 1)]) for i in range(2)])
+
+    def own_chip(e):
+        m = lists(e)
+        need("v", m, *XL)
+        need("s", m, *XL)
+        a = gather_v(sb_at(4 + e), xs, list_of(T.goff, e, im))
+        own_mark.append(gather_s(slot_at(e), xs, list_of(T.goff, e, io)))
+        need("g", a)
+        send([(cores[mate], sb_at(4 + e), slot_at(e), arr[e], on_r)])
+
+    if is_rank:
+        n["lst0"] = n["lst1"] = len(off)
+        dests = table[lister][2]
+        own_chip(0)
         for e in range(2):
-            v(vec.memset(land[e][:, N * CAPP:LANDW], 0.0))
-        need("v", g_mq)
-        i8 = T.i240[:, 112:120]
-        v(vec.tensor_scalar(T.M1[:, :], i8, pk, None, A.is_le))
-        v(vec.tensor_scalar(T.M2[:, :], i8, pk, -1.0, A.is_equal, A.mult))
-        v(vec.tensor_scalar(T.Zr[:, :], T.mq[:, :], pq, None, A.is_equal))
-        v(vec.tensor_scalar(T.P0h[:, :], T.P0[:, :], pq, None, A.add))
-        m = v(vec.tensor_scalar(T.P1[:, :], T.P0[:, :], pq, None, A.add))
-        n_src = 2 * 3 * hlf + len(on)
+            pair(e, T.gpl, ("lst%d" % e, len(off)), dests)
+        own_chip(1)
+    else:
+        for e in range(2):
+            if is_list:
+                need("g", lists(e))
+                w = slice(64 * e, 64 * e + 64)
+                send([(c_r, T.goff[:, w], T.gpl[:, w], T.sem["lst%d" % e], off)])
+            else:
+                pair(e, T.goff, lists(e), grp)
+
+    if is_rank:
+        n_src = 2 * 3 * hlf + len(on_r)
         n["cnt"] = n["arr0"] = n["arr1"] = n_src
-        need("v", m, s_own, ("cnt", n_src))
-        for e in range(2):
-            v(vec.tensor_tensor(T.TT[:, 16 * e:16 * e + 8], T.CT[:, e::4], T.M1[:, :], A.mult))
-            m = v(vec.tensor_tensor(T.TT[:, 16 * e + 8:16 * e + 16], T.CT[:, e::4], T.M2[:, :], A.mult))
+        need("p", v_rc)
+        mm(T.tabp[:, 0:2 * NC], T.I16[:, :], T.P0h[:, :], True, False)
+        need("v", v_rc, s_own, ("cnt", n_src))
+        v(vec.tensor_tensor(T.TT[:, 0:4 * N], T.CT[:, :], T.M1[:, :], A.mult))
+        m = v(vec.tensor_tensor(T.TT[:, 4 * N:8 * N], T.CT[:, :], T.M2[:, :], A.mult))
         need("v", m)
         for e in range(2):
-            v(vec.tensor_reduce(T.SD[:, 2 * e + 4:2 * e + 5], T.TT[:, 16 * e + 8:16 * e + 16], X, A.add))
-            m = v(vec.tensor_reduce(T.SD[:, 2 * e:2 * e + 1], T.TT[:, 16 * e:16 * e + 8], X, A.add))
-        need("v", m)
+            m = v(vec.tensor_reduce(T.SD[:, 2 + e:3 + e], T.TT[:, 4 * N + e::4], X, A.add))
         for e in range(2):
-            m = v(vec.tensor_scalar(T.SD[:, 2 * e + 1:2 * e + 2], T.SD[:, 2 * e + 4:2 * e + 5], float(CAPP), None, A.add))
+            m2 = v(vec.tensor_reduce(T.SD[:, e:e + 1], T.TT[:, e:4 * N:4], X, A.add))
         need("v", m)
+        m = v(vec.tensor_scalar(T.SD[:, 4:6], T.SD[:, 2:4], float(CAPP), None, A.add))
+        need("v", m, m2)
         for e in range(2):
-            m = v(vec.tensor_scalar(T.R[:, NC * e:NC * (e + 1)], T.P1[:, :], T.SD[:, 2 * e:2 * e + 1],
-                                    T.SD[:, 2 * e + 1:2 * e + 2], A.is_ge, A.mult))
+            m = v(vec.tensor_scalar(T.R[:, NC * e:NC * (e + 1)], T.P1[:, :], T.SD[:, e:e + 1], T.SD[:, 4 + e:5 + e], A.is_ge, A.mult))
         need("p", m)
-        for e in range(2):
-            mm(T.tabp[:, NC * e:NC * (e + 1)], T.I16[:, :], T.P0h[:, :], True, False)
-            ins = mm(T.tabp[:, NC * e:NC * (e + 1)], T.Zr[:, :], T.R[:, NC * e:NC * (e + 1)], False, True)
-        p_t = pe(ins)
+        p_t = pe(mm(T.tabp[:, 0:2 * NC], T.Zr[:, :], T.R[:, :], False, True))
         need("v", p_t)
-        v_yt = v(vec.tensor_copy(T.ytab[:, :], T.tabp[:, 0:2 * NC]))
+        v_yt = v(vec.tensor_scalar(T.ytab[:, :], T.tabp[:, 0:2 * NC], float(N * CAPP), None, A.min))
         need("v", v_yt)
         need("s", v_yt)
 

@@ -3,8 +3,6 @@ from concourse.mybir import AluOpType, ActivationFunctionType, AxisListType
 
 WORLD, N, COLS, EL, CAP, CAPP = 256, 8, 4096, 2, 1920, 512
 LANDW = N * CAPP + 16
-PIECES = (0, 1536, 2816, 4096)
-NP = len(PIECES) - 1
 NC = CAP // 16
 
 
@@ -24,7 +22,7 @@ SCRATCH = {
     "O": sb(128, "bfloat16"), "S": sb(136, "bfloat16"), "V": sb(128, "float16"),
     "Cn": sb(8, "bfloat16"), "CS": sb(8),
     "dat": sb(512, "bfloat16"), "win": sb(5 * CAPP, "bfloat16"),
-    "soff": sb(32, "uint16"), "goff": sb(128, "uint16"), "gpl": sb(128, "uint16"),
+    "soff": sb(32, "uint16"), "goff": sb(128, "uint16"), "gown": sb(128, "uint16"),
     "sb": sb(6 * CAPP, "bfloat16"),
     "CT": sb(4 * N),
     "land0": sb(LANDW, "bfloat16"), "land1": sb(LANDW, "bfloat16"),
@@ -33,8 +31,7 @@ SCRATCH = {
     "R": sb(2 * NC, "float16"), "ytab": sb(2 * NC, "uint16"), "ys": sb(EL * CAP, "bfloat16"),
     "pos": PS, "tgt": PS, "cntp": PS, "lstA": PS, "lstB": PS, "tabp": PS,
 }
-SEMAPHORES = (["sv", "ss", "sp", "sg", "lex", "rex", "cnt", "arr0", "arr1", "lst0", "lst1", "sent", "stored"]
-              + ["lx%d" % h for h in range(NP)] + ["rx%d" % h for h in range(NP)])
+SEMAPHORES = ["sv", "ss", "sp", "sg", "lex", "lx", "rex", "rx", "cnt", "arr0", "arr1", "lst0", "lst1", "sent", "stored"]
 CACHE = {}
 
 
@@ -48,26 +45,26 @@ def roles(T, topo):
         chips.setdefault(place(c), []).append(r)
     out, who = {}, {}
 
-    def take(part, r, grp, fits):
-        c = cores[r]
+    def take(part, r, grp):
+        c, d = cores[r], cores[grp[0]]
         for h in range(WORLD):
-            if h not in cores and h not in out and topo.die(h) == topo.die(c) and topo.may_write(h, cores[grp[0]]) and fits(h):
+            if h in cores or h in out or topo.die(h) != topo.die(c) or not topo.may_write(h, d):
+                continue
+            if topo.mates(h, d) and topo.same_plane(c, h) if part == "far" else place(h) == place(c):
                 out[h], who[part, r] = (part, r, grp), h
                 return
-    plane = {}
+    own = {}
     for r, c in enumerate(cores):
         for pl, grp in chips.items():
             d = cores[grp[0]]
             if pl == place(c):
-                out[c] = ("rank", r, grp)
+                own[r] = grp
             elif topo.same_plane(c, d):
-                plane[r] = grp
-            elif topo.host(c) == topo.host(d):
-                take("far", r, grp, lambda h: topo.mates(h, d) and topo.same_plane(c, h))
+                out[c] = ("rank", r, grp)
             else:
-                take("near", r, grp, lambda h: place(h) == place(c))
-    for r, c in enumerate(cores):
-        take("list", r, plane[r], lambda h: place(h) == place(c))
+                take("far" if topo.host(c) == topo.host(d) else "diag", r, grp)
+    for r in range(N):
+        take("list", r, own[r])
     return out, who
 
 
@@ -121,29 +118,26 @@ def rank_program(g, core, T, topo):
 
     vec, sca, ten = g.vector, g.scalar, g.tensor
     mm = ten.matmul
-    far, near, lister = who["far", r], who["near", r], who["list", r]
+    far, diag, lister = who["far", r], who["diag", r], who["list", r]
     c_r = cores[r]
-    off_r = bits(topo.mask(c_r, far))
-    on_r = [b for b in bits(topo.mask(c_r, near)) if b not in off_r]
-    half = len(on_r) // 2
-    off = off_r if is_rank else bits(topo.mask(core, cores[grp[0]]))
+    off = bits(topo.mask(diag, cores[table[diag][2][0]]))
+    on = [b for b in bits(topo.mask(c_r, diag)) if b not in off]
     hlf = len(off) // 2
-    mate = [d for d in table[c_r][2] if d != r][0]
+    own = table[lister][2]
+    mate = [d for d in own if d != r][0]
+    io, im = own.index(r), own.index(mate)
+    ex, xs = T.exs[:, :], T.xs[:, :]
 
-    XP = [T.xs[:, PIECES[h]:PIECES[h + 1]] for h in range(NP)]
-    XL = []
     if is_rank:
         for k in range(8):
             eng = g.sync if k % 2 == 0 else g.scalar
             EXL = did("lex", eng.dma_start(T.ext[16 * k:16 * k + 16, :], T.ex[:, :]), 16)
-        for h in range(NP):
-            eng = g.sync if h % 2 == 0 else g.scalar
-            XL.append(did("lx%d" % h, eng.dma_start(XP[h], T.x[:, PIECES[h]:PIECES[h + 1]]), 16))
+        XL = did("lx", g.sync.dma_start(xs, T.x[:, :]), 16)
     else:
-        n["rex"] = len(off_r) if part == "far" else half
-        for h in range(0 if is_list else NP):
-            n["rx%d" % h] = len(off_r) if part == "far" else len(on_r) if h else len(off_r + on_r)
-            XL.append(("rx%d" % h, n["rx%d" % h]))
+        n["rex"] = len(off) if part == "far" else hlf
+        if not is_list:
+            n["rx"] = len(off) if part == "far" else len(on)
+            XL = ("rx", n["rx"])
 
     v(vec.memset(T.win[:, CAPP:5 * CAPP], 0.0))
     if is_rank:
@@ -154,33 +148,17 @@ def rank_program(g, core, T, topo):
         EXS = ("rex", n["rex"])
 
     ok = {"allow_small_or_imprecise_dtypes": True}
-
-    def x_on(h):
-        w, sem = XP[h], T.sem["rx%d" % h]
-        if is_rank:
-            need("g", XL[h])
-            if h == 0:
-                send([(near, w, w, sem, off_r + on_r)])
-            else:
-                send([(far, w, w, sem, off_r), (near, w, w, sem, on_r)])
-        elif part == "near" and h == 0:
-            need("g", XL[h])
-            send([(far, w, w, sem, off_r)])
-
     g_pi = gp(g.iota(T.PI[:, 0:1], [[1, 1]], 0, 1))
     gp(g.iota(T.i176[:, :], [[1, 176]], -48, 0, **ok))
     g_mk = gp(g.iota(T.mk[:, :], [[0, 2], [1, 4], [0, 16]], 0, 0, **ok))
     if is_rank:
         need("g", EXS)
-        ex = T.exs[:, :]
-        send([(far, ex, ex, T.sem.rex, off_r), (near, ex, ex, T.sem.rex, on_r[:half]), (lister, ex, ex, T.sem.rex, on_r[half:])])
-        x_on(0)
-        x_on(1)
+        send([(far, ex, ex, T.sem.rex, off), (diag, ex, ex, T.sem.rex, on[:hlf]), (lister, ex, ex, T.sem.rex, on[hlf:])])
+        need("g", XL)
+        send([(far, xs, xs, T.sem.rx, off), (diag, xs, xs, T.sem.rx, on)])
     g_JC = gp(g.iota(T.JC[:, :], [[0, 4], [-16, 32]], 0, 0, **ok))
     g_A = gp(g.iota(T.A[:, :], [[32, 8], [1, 16]], 0, 0, **ok))
     g_kk = gp(g.iota(T.kk[:, :], [[1, 2], [2, 4]], 0, 0, **ok))
-    for h in range(2 if is_rank else 0, NP):
-        x_on(h)
     if is_rank:
         gp(g.iota(T.P0[:, :], [[0, 2], [16, NC]], 0, 0, **ok))
         gp(g.iota(T.r32[:, :], [[1, N], [0, 4]], 0, 0, **ok))
@@ -267,14 +245,8 @@ def rank_program(g, core, T, topo):
     need("s", p_cnt)
     s_CS = s(sca.activation(T.CS[:, :], T.cntp[:, 0:8], F.Copy))
     slot = T.CT[:, 4 * r:4 * r + 4]
-    if is_rank:
-        io, im = grp.index(r), grp.index(mate)
-        s_own = s(sca.activation(slot, T.cntp[:, 4 * io:4 * io + 4], F.Copy))
     need("g", s_CS)
-    if is_rank:
-        send([(cores[mate], T.CS[:, 4 * im:4 * im + 4], slot, T.sem.cnt, on_r)])
-    else:
-        send([(cores[grp[i]], T.CS[:, 4 * i:4 * i + 4], slot, T.sem.cnt, off[hlf * i:hlf * (i + 1)]) for i in range(2)])
+    send([(cores[grp[i]], T.CS[:, 4 * i:4 * i + 4], slot, T.sem.cnt, off[hlf * i:hlf * (i + 1)]) for i in range(2)])
 
     need("p", v_sc)
     p_l = []
@@ -300,7 +272,6 @@ def rank_program(g, core, T, topo):
     def gather_s(out, w, o):
         return s(sca.activation(out, w.indirect(o), F.Identity, bias=-0.0, scale=1.0))
 
-    xs = T.xs[:, :]
     land, arr = [T.land0, T.land1], [T.sem.arr0, T.sem.arr1]
     own_mark = []
 
@@ -317,45 +288,43 @@ def rank_program(g, core, T, topo):
     def slot_at(e):
         return land[e][:, CAPP * r:CAPP * (r + 1)]
 
-    def pair(e, buf, mark, dests):
-        need("v", mark, *XL)
-        need("s", mark, *XL)
-        a = gather_v(sb_at(2 * e), xs, list_of(buf, e, 0))
-        b = gather_s(sb_at(2 * e + 1), xs, list_of(buf, e, 1))
+    def pair(e):
+        m = lists(e)
+        need("v", m, XL)
+        need("s", m, XL)
+        a = gather_v(sb_at(2 * e), xs, list_of(T.goff, e, 0))
+        b = gather_s(sb_at(2 * e + 1), xs, list_of(T.goff, e, 1))
         need("g", a, b)
-        send([(cores[dests[i]], sb_at(2 * e + i), slot_at(e), arr[e], off[hlf * i:hlf * (i + 1)]) for i in range(2)])
+        send([(cores[grp[i]], sb_at(2 * e + i), slot_at(e), arr[e], off[hlf * i:hlf * (i + 1)]) for i in range(2)])
 
     def own_chip(e):
-        m = lists(e)
-        need("v", m, *XL)
-        need("s", m, *XL)
-        a = gather_v(sb_at(4 + e), xs, list_of(T.goff, e, im))
-        own_mark.append(gather_s(slot_at(e), xs, list_of(T.goff, e, io)))
+        m = ("lst%d" % e, n["lst%d" % e])
+        need("v", m, XL)
+        need("s", m, XL)
+        a = gather_v(sb_at(4 + e), xs, list_of(T.gown, e, im))
+        own_mark.append(gather_s(slot_at(e), xs, list_of(T.gown, e, io)))
         need("g", a)
-        send([(cores[mate], sb_at(4 + e), slot_at(e), arr[e], on_r)])
+        send([(cores[mate], sb_at(4 + e), slot_at(e), arr[e], on)])
+
+    for e in range(2):
+        if is_list:
+            need("g", lists(e))
+            w = slice(64 * e, 64 * e + 64)
+            send([(c_r, T.goff[:, w], T.gown[:, w], T.sem["lst%d" % e], off)])
+        else:
+            pair(e)
 
     if is_rank:
         n["lst0"] = n["lst1"] = len(off)
-        dests = table[lister][2]
-        own_chip(0)
         for e in range(2):
-            pair(e, T.gpl, ("lst%d" % e, len(off)), dests)
-        own_chip(1)
-    else:
-        for e in range(2):
-            if is_list:
-                need("g", lists(e))
-                w = slice(64 * e, 64 * e + 64)
-                send([(c_r, T.goff[:, w], T.gpl[:, w], T.sem["lst%d" % e], off)])
-            else:
-                pair(e, T.goff, lists(e), grp)
-
-    if is_rank:
-        n_src = 2 * 3 * hlf + len(on_r)
-        n["cnt"] = n["arr0"] = n["arr1"] = n_src
+            own_chip(e)
+        n_src = 2 * 3 * hlf + len(on)
+        n_cnt = 2 * 4 * hlf
+        n["arr0"] = n["arr1"] = n_src
+        n["cnt"] = n_cnt
         need("p", v_rc)
         mm(T.tabp[:, 0:2 * NC], T.I16[:, :], T.P0h[:, :], True, False)
-        need("v", v_rc, s_own, ("cnt", n_src))
+        need("v", v_rc, ("cnt", n_cnt))
         v(vec.tensor_tensor(T.TT[:, 0:4 * N], T.CT[:, :], T.M1[:, :], A.mult))
         m = v(vec.tensor_tensor(T.TT[:, 4 * N:8 * N], T.CT[:, :], T.M2[:, :], A.mult))
         need("v", m)

from concourse.bass import DstId, RemoteDMATransfer
from concourse.mybir import AluOpType, ActivationFunctionType, AxisListType

WORLD, N, COLS, EL, CAP, CAPP = 256, 8, 4096, 2, 1920, 512
LANDW = N * CAPP + 16
NC = CAP // 16


def sb(n, dtype="float32"):
    return ("sbuf", [128, n], dtype)


PS = ("psum", [128, 512], "float32")
SCRATCH = {
    "ext": sb(256, "int32"), "exs": sb(128, "bfloat16"),
    "xs": sb(COLS, "bfloat16"),
    "PI": sb(8, "int32"), "PF": sb(8), "W": sb(16),
    "i176": sb(176), "mk": sb(128), "JC": sb(128), "A": sb(128, "bfloat16"), "kk": sb(8),
    "mask8": sb(8, "bfloat16"), "Z2": sb(176, "float16"), "Z3": sb(176, "bfloat16"), "Zq": sb(144, "bfloat16"),
    "ones": sb(128, "bfloat16"), "B": sb(128, "bfloat16"), "GT": sb(128, "bfloat16"), "L": sb(128, "bfloat16"),
    "I16": sb(128, "float16"), "Jneg": sb(128, "float16"), "JT": sb(32, "float16"),
    "O": sb(128, "bfloat16"), "S": sb(136, "bfloat16"), "V": sb(128, "float16"),
    "Cn": sb(8, "bfloat16"), "CS": sb(8),
    "dat": sb(512, "bfloat16"), "win": sb(5 * CAPP, "bfloat16"),
    "soff": sb(32, "uint16"), "goff": sb(128, "uint16"), "gown": sb(128, "uint16"),
    "sb": sb(6 * CAPP, "bfloat16"),
    "CT": sb(4 * N),
    "land0": sb(LANDW, "bfloat16"), "land1": sb(LANDW, "bfloat16"),
    "P0": sb(2 * NC), "P1": sb(NC), "P0h": sb(2 * NC, "float16"), "mq": sb(128), "r32": sb(4 * N), "Zr": sb(128, "float16"),
    "M1": sb(4 * N), "M2": sb(4 * N), "TT": sb(8 * N), "SD": sb(8),
    "R": sb(2 * NC, "float16"), "ytab": sb(2 * NC, "uint16"), "ys": sb(EL * CAP, "bfloat16"),
    "pos": PS, "tgt": PS, "cntp": PS, "lstA": PS, "lstB": PS, "tabp": PS,
}
SEMAPHORES = ["sv", "ss", "sp", "sg", "lex", "lx", "rex", "rx", "cnt", "arr0", "arr1", "lst0", "lst1", "sent", "stored"]
CACHE = {}


def roles(T, topo):
    cores = T.cores

    def place(c):
        return (topo.host(c), topo.chip(c))
    chips = {}
    for r, c in enumerate(cores):
        chips.setdefault(place(c), []).append(r)
    out, who = {}, {}

    def take(part, r, grp):
        c, d = cores[r], cores[grp[0]]
        for h in range(WORLD):
            if h in cores or h in out or topo.die(h) != topo.die(c) or not topo.may_write(h, d):
                continue
            if topo.mates(h, d) and topo.same_plane(c, h) if part == "far" else place(h) == place(c):
                out[h], who[part, r] = (part, r, grp), h
                return
    own = {}
    for r, c in enumerate(cores):
        for pl, grp in chips.items():
            d = cores[grp[0]]
            if pl == place(c):
                own[r] = grp
            elif topo.same_plane(c, d):
                out[c] = ("rank", r, grp)
            else:
                take("far" if topo.host(c) == topo.host(d) else "diag", r, grp)
    for r in range(N):
        take("list", r, own[r])
    return out, who


def bits(m):
    return [1 << i for i in range(16) if m >> i & 1]


def rank_program(g, core, T, topo):
    if "roles" not in CACHE:
        CACHE["roles"] = roles(T, topo)
    table, who = CACHE["roles"]
    if core not in table:
        return
    part, r, grp = table[core]
    cores = T.cores
    is_rank, is_list = part == "rank", part == "list"
    A, X, F = AluOpType, AxisListType.X, ActivationFunctionType
    q = {"v": g.vector, "s": g.scalar, "p": g.tensor, "g": g, "y": g.sync}
    n, seen = {}, {}

    def did(name, ins, k=1):
        ins.then_inc(T.sem[name], k)
        n[name] = n.get(name, 0) + k
        return (name, n[name])

    def need(k, *marks):
        for name, val in marks:
            if seen.get((k, name), 0) < val:
                q[k].wait_ge(T.sem[name], val)
                seen[(k, name)] = val

    def v(ins):
        return did("sv", ins)

    def s(ins):
        return did("ss", ins)

    def pe(ins):
        return did("sp", ins)

    def gp(ins):
        return did("sg", ins)

    def send(parts):
        ts = []
        for d, a, b, sem, eng in parts:
            rid, pnc = topo.addr(d, core)
            n["sent"] = n.get("sent", 0) + len(eng)
            ts.append(RemoteDMATransfer(dst_ids=[DstId(rid=rid, pnc=pnc)], dma_engine_mask=sum(eng), remote_sem=sem, src=a, dst=b))
        g.remote_dma_fused(ts, local_sem=T.sem.sent)

    vec, sca, ten = g.vector, g.scalar, g.tensor
    mm = ten.matmul
    far, diag, lister = who["far", r], who["diag", r], who["list", r]
    c_r = cores[r]
    off = bits(topo.mask(diag, cores[table[diag][2][0]]))
    on = [b for b in bits(topo.mask(c_r, diag)) if b not in off]
    hlf = len(off) // 2
    own = table[lister][2]
    mate = [d for d in own if d != r][0]
    io, im = own.index(r), own.index(mate)
    ex, xs = T.exs[:, :], T.xs[:, :]

    if is_rank:
        for k in range(8):
            eng = g.sync if k % 2 == 0 else g.scalar
            EXL = did("lex", eng.dma_start(T.ext[16 * k:16 * k + 16, :], T.ex[:, :]), 16)
        XL = did("lx", g.sync.dma_start(xs, T.x[:, :]), 16)
    else:
        n["rex"] = len(off) if part == "far" else hlf
        if not is_list:
            n["rx"] = len(off) if part == "far" else len(on)
            XL = ("rx", n["rx"])

    v(vec.memset(T.win[:, CAPP:5 * CAPP], 0.0))
    if is_rank:
        need("v", EXL)
        v(vec.tensor_copy(T.exs[0:64, :], T.ext[0:64, 0::2]))
        EXS = v(vec.tensor_copy(T.exs[64:128, :], T.ext[64:128, 1::2]))
    else:
        EXS = ("rex", n["rex"])

    ok = {"allow_small_or_imprecise_dtypes": True}
    g_pi = gp(g.iota(T.PI[:, 0:1], [[1, 1]], 0, 1))
    gp(g.iota(T.i176[:, :], [[1, 176]], -48, 0, **ok))
    g_mk = gp(g.iota(T.mk[:, :], [[0, 2], [1, 4], [0, 16]], 0, 0, **ok))
    if is_rank:
        need("g", EXS)
        send([(far, ex, ex, T.sem.rex, off), (diag, ex, ex, T.sem.rex, on[:hlf]), (lister, ex, ex, T.sem.rex, on[hlf:])])
        need("g", XL)
        send([(far, xs, xs, T.sem.rx, off), (diag, xs, xs, T.sem.rx, on)])
    g_JC = gp(g.iota(T.JC[:, :], [[0, 4], [-16, 32]], 0, 0, **ok))
    g_A = gp(g.iota(T.A[:, :], [[32, 8], [1, 16]], 0, 0, **ok))
    g_kk = gp(g.iota(T.kk[:, :], [[1, 2], [2, 4]], 0, 0, **ok))
    if is_rank:
        gp(g.iota(T.P0[:, :], [[0, 2], [16, NC]], 0, 0, **ok))
        gp(g.iota(T.r32[:, :], [[1, N], [0, 4]], 0, 0, **ok))
        g_mq = gp(g.iota(T.mq[:, :], [[0, 8], [1, 16]], 0, 0, **ok))

    v(vec.memset(T.ones[:, :], 1.0))
    v(vec.memset(T.Zq[:, :], 0.0))
    v(vec.memset(T.S[:, 0:1], 0.0))
    need("v", g_pi)
    pi = T.PI[:, 0:1]
    v(vec.tensor_scalar(T.PI[:, 1:2], pi, 4, None, A.arith_shift_right))
    v(vec.tensor_scalar(T.PI[:, 2:3], pi, 15, None, A.bitwise_and))
    v(vec.tensor_scalar(T.PI[:, 3:4], pi, 79, None, A.bitwise_and))
    v(vec.tensor_scalar(T.PI[:, 4:5], pi, 4, 3, A.arith_shift_right, A.bitwise_and))
    v(vec.tensor_scalar(T.PI[:, 5:6], pi, 4, 1, A.arith_shift_right, A.bitwise_and))
    v(vec.tensor_scalar(T.PI[:, 6:7], pi, 5, 1, A.arith_shift_right, A.bitwise_and))
    m = v(vec.tensor_scalar(T.PI[:, 7:8], pi, 6, None, A.arith_shift_right))
    need("v", m)
    m = v(vec.tensor_copy(T.PF[:, :], T.PI[:, :]))
    need("v", m)
    pf, pr, pq, ph, pk, p_i, p_e, p_h = [T.PF[:, j:j + 1] for j in range(8)]
    w0, w1, w2, kw, eb, ta, tb, wu, wg, d1, d2, d3 = [T.W[:, j:j + 1] for j in range(12)]
    v(vec.tensor_scalar(w0, pq, 0.0, None, A.is_equal))
    v(vec.tensor_scalar(w1, pq, 1.0, None, A.is_equal))
    v(vec.tensor_scalar(w2, pq, 2.0, None, A.is_equal))
    v(vec.tensor_scalar(kw, pk, float(CAPP), float(CAPP), A.mult, A.add))
    v(vec.tensor_scalar(eb, p_i, 2.0, p_e, A.mult, A.add))
    m = v(vec.tensor_scalar(ta, pk, 1024.0, None, A.mult))
    need("v", g_mk)
    mI = T.i176[:, 48:176]
    v(vec.tensor_scalar(T.B[:, :], T.mk[:, :], pk, None, A.is_equal))
    v(vec.tensor_scalar(T.GT[:, :], mI, pf, None, A.is_gt))
    v(vec.tensor_scalar(T.I16[:, :], mI, pf, None, A.is_equal))
    v(vec.tensor_scalar(T.Z2[:, :], T.i176[:, :], ph, None, A.is_equal))
    need("v", m)
    v(vec.tensor_scalar(T.Z3[:, :], T.i176[:, :], ph, kw, A.is_equal, A.mult))
    v(vec.tensor_scalar(tb, p_h, 16.0, ta, A.mult, A.add))
    v(vec.tensor_scalar(wu, w1, 256.0, w0, A.mult, A.add))
    v(vec.tensor_scalar(d1, w1, 1.0, w2, A.mult, A.add))
    v(vec.tensor_scalar(d2, w1, 2.0, w2, A.mult, A.add))
    m = v_d = v(vec.tensor_scalar(d3, w1, 3.0, w2, A.mult, A.add))
    need("v", m)
    v(vec.tensor_tensor(T.L[:, :], T.GT[:, :], T.B[:, :], A.mult))
    m = v(vec.tensor_scalar(wg, tb, w2, wu, A.mult, A.add))
    need("v", g_JC)
    v(vec.tensor_scalar(T.Jneg[:, :], T.JC[:, :], pq, None, A.subtract))
    v_JT = v(vec.tensor_scalar(T.JT[:, :], T.JC[:, 0:32], -1.0, pq, A.mult, A.add))
    need("v", m)
    v(vec.tensor_scalar(T.Zq[:, 15::16], T.ones[:, 0:9], wg, None, A.mult))
    need("v", g_kk)
    v_c = v(vec.tensor_scalar(T.mask8[:, :], T.kk[:, :], pk, None, A.is_equal))
    need("s", g_A, v_d)
    for d, bias in enumerate((w2, d1, d2, d3)):
        s_dat = s(sca.activation(T.dat[:, 128 * d:128 * d + 128], T.A[:, :], F.Identity, bias=bias, scale=w0))

    need("v", EXS, v_c)
    v_O = v(vec.tensor_scalar(T.O[:, :], T.exs[:, :], float(EL * grp[0]), eb, A.subtract, A.is_equal))
    need("v", v_O)
    v_S = v(vec.tensor_tensor_scan(T.S[:, 1:129], T.O[:, :], T.O[:, :], 0.0, A.add, A.max))
    need("v", v_S)
    v(vec.tensor_scalar(T.Cn[:, :], T.mask8[:, :], T.S[:, 128:129], None, A.mult))

    need("p", v_JT)
    mm(T.tgt[:, 0:32], T.I16[:, :], T.JT[:, :], True, False)
    mm(T.pos[:, 0:128], T.I16[:, :], T.Jneg[:, :], True, False)
    need("p", v_O)
    mm(T.pos[:, 0:128], T.L[:, :], T.O[:, :], False, False)
    need("p", v_S)
    p_pos = pe(mm(T.pos[:, 0:128], T.B[:, :], T.S[:, 0:128], False, True))
    for b in range(4):
        mm(T.tgt[:, 0:32], T.Z3[:, 48 - 16 * b:176 - 16 * b], T.O[:, 32 * b:32 * b + 32], False, False)
    need("v", p_pos)
    v_V = v(vec.tensor_tensor(T.V[:, :], T.O[:, :], T.pos[:, 0:128], A.mult))
    need("p", v_V)
    for b in range(4):
        ins = mm(T.tgt[:, 0:32], T.Z2[:, 48 - 16 * b:176 - 16 * b], T.V[:, 32 * b:32 * b + 32], False, b == 3)
    p_tgt = pe(ins)
    p_cnt = pe(mm(T.cntp[:, 0:8], T.ones[:, :], T.Cn[:, :], True, True))
    need("v", p_tgt)
    v_so = v(vec.tensor_copy(T.soff[:, :], T.tgt[:, 0:32]))
    need("v", v_so, s_dat)
    v_sc = v(vec.tensor_copy(T.win[:, :].indirect(T.soff[:, 0:32]), T.dat[:, :]))

    need("s", p_cnt)
    s_CS = s(sca.activation(T.CS[:, :], T.cntp[:, 0:8], F.Copy))
    slot = T.CT[:, 4 * r:4 * r + 4]
    need("g", s_CS)
    send([(cores[grp[i]], T.CS[:, 4 * i:4 * i + 4], slot, T.sem.cnt, off[hlf * i:hlf * (i + 1)]) for i in range(2)])

    need("p", v_sc)
    p_l = []
    for e, bank in enumerate((T.lstA, T.lstB)):
        a = CAPP + 2 * CAPP * e
        for j in range(16):
            ins = mm(bank[:, 0:64], T.Zq[:, 15 - j:143 - j], T.win[:, a + j:a + 2 * CAPP:16], j == 0, j == 15)
        p_l.append(pe(ins))

    if is_rank:
        v(vec.memset(T.land0[:, N * CAPP:LANDW], 0.0))
        v(vec.memset(T.land1[:, N * CAPP:LANDW], 0.0))
        need("v", g_mq)
        v(vec.tensor_scalar(T.M1[:, :], T.r32[:, :], pr, None, A.is_le))
        v(vec.tensor_scalar(T.M2[:, :], T.r32[:, :], pr, -1.0, A.is_equal, A.mult))
        v(vec.tensor_scalar(T.Zr[:, :], T.mq[:, :], pq, None, A.is_equal))
        v(vec.tensor_scalar(T.P1[:, :], T.P0[:, 0:NC], pq, None, A.add))
        v_rc = v(vec.tensor_scalar(T.P0h[:, :], T.P0[:, :], pq, None, A.add))

    def gather_v(out, w, o):
        return v(vec.tensor_copy(out, w.indirect(o)))

    def gather_s(out, w, o):
        return s(sca.activation(out, w.indirect(o), F.Identity, bias=-0.0, scale=1.0))

    land, arr = [T.land0, T.land1], [T.sem.arr0, T.sem.arr1]
    own_mark = []

    def lists(e):
        need("v", p_l[e])
        return v(vec.tensor_copy(T.goff[:, 64 * e:64 * e + 64], (T.lstA, T.lstB)[e][:, 0:64]))

    def list_of(buf, e, i):
        return buf[:, 64 * e + 32 * i:64 * e + 32 * i + 32]

    def sb_at(j):
        return T.sb[:, CAPP * j:CAPP * (j + 1)]

    def slot_at(e):
        return land[e][:, CAPP * r:CAPP * (r + 1)]

    def pair(e):
        m = lists(e)
        need("v", m, XL)
        need("s", m, XL)
        a = gather_v(sb_at(2 * e), xs, list_of(T.goff, e, 0))
        b = gather_s(sb_at(2 * e + 1), xs, list_of(T.goff, e, 1))
        need("g", a, b)
        send([(cores[grp[i]], sb_at(2 * e + i), slot_at(e), arr[e], off[hlf * i:hlf * (i + 1)]) for i in range(2)])

    def own_chip(e):
        m = ("lst%d" % e, n["lst%d" % e])
        need("v", m, XL)
        need("s", m, XL)
        a = gather_v(sb_at(4 + e), xs, list_of(T.gown, e, im))
        own_mark.append(gather_s(slot_at(e), xs, list_of(T.gown, e, io)))
        need("g", a)
        send([(cores[mate], sb_at(4 + e), slot_at(e), arr[e], on)])

    for e in range(2):
        if is_list:
            need("g", lists(e))
            w = slice(64 * e, 64 * e + 64)
            send([(c_r, T.goff[:, w], T.gown[:, w], T.sem["lst%d" % e], off)])
        else:
            pair(e)

    if is_rank:
        n["lst0"] = n["lst1"] = len(off)
        for e in range(2):
            own_chip(e)
        n_src = 2 * 3 * hlf + len(on)
        n_cnt = 2 * 4 * hlf
        n["arr0"] = n["arr1"] = n_src
        n["cnt"] = n_cnt
        need("p", v_rc)
        mm(T.tabp[:, 0:2 * NC], T.I16[:, :], T.P0h[:, :], True, False)
        need("v", v_rc, ("cnt", n_cnt))
        v(vec.tensor_tensor(T.TT[:, 0:4 * N], T.CT[:, :], T.M1[:, :], A.mult))
        m = v(vec.tensor_tensor(T.TT[:, 4 * N:8 * N], T.CT[:, :], T.M2[:, :], A.mult))
        need("v", m)
        for e in range(2):
            m = v(vec.tensor_reduce(T.SD[:, 2 + e:3 + e], T.TT[:, 4 * N + e::4], X, A.add))
        for e in range(2):
            m2 = v(vec.tensor_reduce(T.SD[:, e:e + 1], T.TT[:, e:4 * N:4], X, A.add))
        need("v", m)
        m = v(vec.tensor_scalar(T.SD[:, 4:6], T.SD[:, 2:4], float(CAPP), None, A.add))
        need("v", m, m2)
        for e in range(2):
            m = v(vec.tensor_scalar(T.R[:, NC * e:NC * (e + 1)], T.P1[:, :], T.SD[:, e:e + 1], T.SD[:, 4 + e:5 + e], A.is_ge, A.mult))
        need("p", m)
        p_t = pe(mm(T.tabp[:, 0:2 * NC], T.Zr[:, :], T.R[:, :], False, True))
        need("v", p_t)
        v_yt = v(vec.tensor_scalar(T.ytab[:, :], T.tabp[:, 0:2 * NC], float(N * CAPP), None, A.min))
        need("v", v_yt)
        need("s", v_yt)

        for e in range(2):
            need("v", own_mark[e], ("arr%d" % e, n_src))
            need("s", own_mark[e], ("arr%d" % e, n_src))
            a = 0
            for w in ([CAP // 2], [CAP // 4, CAP // 4])[e]:
                for k, gather in enumerate((gather_v, gather_s)):
                    c0 = CAP // 2 * k + a
                    lo, hi = CAP * e + c0, CAP * e + c0 + w
                    m = gather(T.ys[:, lo:hi], land[e][:, :], T.ytab[:, lo // 16:hi // 16])
                    need("y", m)
                    did("stored", g.sync.dma_start(T.y[:, lo:hi], T.ys[:, lo:hi]), 16)
                a += w

    for name in SEMAPHORES:
        if n.get(name, 0):
            need("g", (name, n[name]))
